import numpy as np
import ml_dtypes


def mxq(x, axis, fmt="e4m3"):
    dtype, down = {"e4m3": (ml_dtypes.float8_e4m3fn, 7), "e5m2": (ml_dtypes.float8_e5m2, 14)}[fmt]
    v = np.moveaxis(np.asarray(x, np.float32).astype(ml_dtypes.bfloat16).astype(np.float64), axis, -1)
    blocks = v.reshape(v.shape[:-1] + (-1, 32))
    amax = np.abs(blocks).max(-1, keepdims=True)
    byte = np.maximum(np.where(amax > 0, np.frexp(amax)[1] - 1 + 127, 0) - down, 1)
    scale = np.exp2(byte - 127.0)
    codes = (blocks / scale).astype(np.float32).astype(dtype).astype(np.float64)
    return np.moveaxis((codes * scale).reshape(v.shape), -1, axis)


WIDE = False


def mx_kscale(k):
    if not WIDE:
        return np.ones(k)
    levels = np.array([10, -10, 5, -5, 0])
    if k % 512:
        return np.exp2(np.random.permutation(np.resize(levels, k // 32))).repeat(32)
    a = np.empty((k // 512, 16))
    for p in range(k // 512):
        a[p, :8] = np.random.permutation(np.resize(levels, 8))
        for g in range(8):
            far = levels[np.abs(levels - a[p, g]) >= 10]
            a[p, g + 8] = far[np.random.randint(len(far))]
    return np.exp2(a.ravel()).repeat(32)


def f64(x):
    return np.asarray(x).astype(np.float64)


def striped(idx):
    return np.tile(idx.reshape(-1, 16).T, (8, 1)).astype(np.uint16)


def unstriped(offs):
    return offs[:16].T.reshape(-1).astype(np.int64)


E2M1 = np.array([0.0, 0.5, 1.0, 1.5, 2.0, 3.0, 4.0, 6.0, -0.0, -0.5, -1.0, -1.5, -2.0, -3.0, -4.0, -6.0])


def pack_weight(w, fmt):
    k, n = w.shape
    w = f64(np.asarray(w, np.float32).astype(ml_dtypes.bfloat16)).reshape(k // 32, 32, n)
    amax = np.abs(w).max(1)
    if fmt == "e4m3":
        byte = np.frexp(amax)[1] - 1 + 127 - 7
    else:
        mant, ex = np.frexp(amax / 6.0)
        byte = np.where(mant > 0.5, ex, ex - 1) + 127
    byte = np.clip(np.where(amax > 0, byte, 1), 1, 254)
    scaled = (w * np.exp2(127.0 - byte)[:, None, :]).reshape(k, n).astype(np.float32)
    by_word = np.ascontiguousarray(scaled.reshape(k // 512, 128, 4, n).transpose(0, 1, 3, 2))
    if fmt == "e4m3":
        words = by_word.astype(ml_dtypes.float8_e4m3fn).view(np.uint8)
    else:
        c = by_word.astype(ml_dtypes.float4_e2m1fn).view(np.uint8) & 0xF
        words = (c[..., 0::2] | (c[..., 1::2] << 4)).reshape(k // 512, 128, 2 * n)
    return np.ascontiguousarray(words), np.ascontiguousarray(byte.astype(np.uint8).reshape(k // 512, 16, n))


def unpack_weight(words, scales, fmt):
    g, _, n = scales.shape
    words = np.ascontiguousarray(words).reshape(g, 128, n, -1)
    if fmt == "e4m3":
        vals = words.view(ml_dtypes.float8_e4m3fn).astype(np.float64)
    else:
        nib = np.empty((g, 128, n, 4), np.uint8)
        nib[..., 0::2] = words & 0xF
        nib[..., 1::2] = words >> 4
        vals = E2M1[nib]
    vals = vals * np.repeat(np.exp2(scales.astype(np.float64) - 127.0), 8, axis=1)[..., None]
    return vals.transpose(0, 1, 3, 2).reshape(g * 512, n)


def gelu(v):
    return 0.5 * v * (1.0 + np.tanh(np.sqrt(2.0 / np.pi) * (v + 0.044715 * v**3)))


def bf(x):
    return np.asarray(x, np.float32).astype(ml_dtypes.bfloat16)


def planes(Y):
    n, m = Y.shape
    b = f64(bf(Y)).reshape(n // 32, 32, m)
    amax = np.abs(b).max(1)
    byte = np.clip(np.where(amax > 0, np.frexp(amax)[1] - 1 + 127 - 7, 1), 1, 254)
    codes = (b * np.exp2(127.0 - byte)[:, None, :]).reshape(n, m).astype(np.float32).astype(ml_dtypes.float8_e4m3fn).view(np.uint8)
    words = codes.reshape(n // 512, 128, 4, m).transpose(0, 1, 3, 2)
    return np.ascontiguousarray(words), np.ascontiguousarray(byte.astype(np.uint8).reshape(n // 512, 16, m))


K, H, N, T, S = 1024, 1024, 512, 4096, 1024

def setup_inputs():
    n = np.random.standard_normal
    s = mx_kscale(K)[:, None]
    u = mx_kscale(H)[:, None]
    d = np.exp(0.8 * n(N))
    tab_words, tab_scales = pack_weight(n((K, T)) * s, "e4m3")
    w1_words, w1_scales = pack_weight(n((K, H)) / np.sqrt(K) / s, "e2m1")
    w2_words, w2_scales = pack_weight(1.5 * n((H, N)) / np.sqrt(H) * d / u, "e4m3")
    return {
        "tab_words": tab_words, "tab_scales": tab_scales,
        "offs": striped(np.random.permutation(T)[:S]),
        "w1_words": w1_words, "w1_scales": w1_scales,
        "w2_words": w2_words, "w2_scales": w2_scales,
        "w3": (1.5 * n((K, N)) / np.sqrt(K) / s).astype(np.float32),
        "pace": (np.exp(0.3 * n((H, S))) * u).astype(np.float32),
        "wgo": np.exp(0.3 * n((128, S))).astype(np.float32),
        "offs2": striped(np.random.permutation(S)),
        "x0": (0.7 * n((N, S)) * d[:, None]).astype(np.float32),
    }

def reference(tab_words, tab_scales, offs, w1_words, w1_scales, w2_words, w2_scales, w3, pace, wgo, offs2, x0):
    v = unpack_weight(tab_words, tab_scales, "e4m3")[:, unstriped(offs)]
    a = unpack_weight(w1_words, w1_scales, "e2m1").T @ v
    h = 0.5 * a * (1.0 + np.tanh(np.sqrt(2.0 / np.pi) * (a + 0.044715 * a ** 3))) * f64(pace)
    b = unpack_weight(w2_words, w2_scales, "e4m3").T @ mxq(h, 0, "e4m3")
    e = mxq(f64(w3), 0, "e4m3").T @ v
    f = b * (1.0 / (1.0 + np.exp(-e)))
    page = np.zeros((N, S))
    page[:, unstriped(offs2)] = np.tile(f64(wgo), (N // 128, 1)) * f
    y = page + f64(x0)
    words, scales = planes(y)
    return y, words, scales

@@ -1,0 +1,289 @@
+from contextlib import ExitStack
+
+import concourse.mybir as mybir
+
+K, H, N, T, S = 1024, 1024, 512, 4096, 1024
+FLOPS = 2 * S * (K * H + H * N + K * N)
+
+F32 = mybir.dt.float32
+BF16 = mybir.dt.bfloat16
+I32 = mybir.dt.int32
+U32 = mybir.dt.uint32
+U16 = mybir.dt.uint16
+U8 = mybir.dt.uint8
+E4M3 = mybir.dt.float8_e4m3fn_x4
+E2M1 = mybir.dt.float4_e2m1fn_x4
+ACT = mybir.ActivationFunctionType
+ALU = mybir.AluOpType
+
+P = 128
+PACK = 4
+KP = P * PACK
+HALF = 512
+LIST_COLS = HALF // 16
+
+
+def tile_list_transcript_corrections_kernel(
+    tc, tab_words, tab_scales, offs, w1_words, w1_scales, w2_words, w2_scales, w3, pace, wgo, offs2, x0,
+    out_0, out_1, out_2,
+):
+    nc = tc.nc
+    with ExitStack() as ctx:
+        lists = ctx.enter_context(tc.tile_pool(name="lists", bufs=1))
+        keep = ctx.enter_context(tc.tile_pool(name="keep", bufs=1))
+        ring = ctx.enter_context(tc.tile_pool(name="ring", bufs=1))
+        psum = ctx.enter_context(tc.psum_pool(name="psum", bufs=8))
+
+        pick = lists.tile([P, S // 16], U16, name="pick")
+        place = lists.tile([P, S // 16], U16, name="place")
+
+        warm = keep.tile([P, 8], F32, name="warm")
+        nc.gpsimd.memset(warm[:], 0.0)
+        warm_out = keep.tile([P, 8], F32, name="warm_out")
+        nc.scalar.activation(warm_out[:], warm[:], ACT.Gelu_apprx_tanh)
+
+        tab_sc = ring.tile([P, T], U8, name="tab_sc", tag="first", bufs=1, align_bytes=64)
+        w1_sc_raw = keep.tile([P, 2 * H], U8, name="w1_sc_raw", align_bytes=64)
+        w2_sc_raw = keep.tile([P, 2 * N], U8, name="w2_sc_raw", align_bytes=64)
+        v_sc = keep.tile([P, 2 * S], U8, name="v_sc", align_bytes=64)
+        nc.vector.memset(w1_sc_raw[:].bitcast(I32), 0)
+        nc.vector.memset(tab_sc[32:64, :].bitcast(I32), 0)
+        nc.vector.memset(tab_sc[64:128, :].bitcast(I32), 0)
+        nc.vector.memset(v_sc[:].bitcast(I32), 0)
+        nc.vector.memset(w2_sc_raw[:].bitcast(I32), 0)
+
+        nc.sync.dma_start(pick[:], offs)
+        nc.sync.dma_start(tab_sc[0:32, :].bitcast(I32), tab_scales.rearrange("a q t -> (a q) t").bitcast(I32))
+        w1_raw = keep.tile([P, 2 * 2 * H], U8, name="w1_raw", align_bytes=64)
+        nc.sync.dma_start(
+            w1_raw[:].bitcast(I32).rearrange("p (a c) -> p a c", a=2),
+            w1_words.bitcast(I32).rearrange("a p c -> p a c"),
+        )
+        for q in range(4):
+            nc.gpsimd.dma_start(
+                w1_sc_raw[32 * q : 32 * q + 4, :].bitcast(I32).rearrange("p (a c) -> p a c", a=2),
+                w1_scales[:, 4 * q : 4 * q + 4, :].bitcast(I32).rearrange("a r c -> r a c"),
+            )
+        tab = []
+        for a in range(2):
+            words = keep.tile([P, T], I32, name="tab%d" % a, align_bytes=64)
+            nc.sync.dma_start(words[:], tab_words[a].rearrange("p t i -> p (t i)").bitcast(I32))
+            tab.append(words)
+
+        picked_sc = keep.tile([P, S], U8, name="picked_sc", align_bytes=64)
+        nc.vector.tensor_copy(picked_sc[:], tab_sc[:].indirect(pick[:]))
+        for a in range(2):
+            for q in range(4):
+                row = 16 * a + 4 * q
+                (nc.gpsimd if a else nc.scalar).dma_start(
+                    v_sc[32 * q : 32 * q + 4, S * a : S * (a + 1)].bitcast(I32),
+                    picked_sc[row : row + 4, :].bitcast(I32),
+                )
+
+        pace_t = {}
+
+        def load_pace(b, h):
+            if (b, h) == (0, 0):
+                tile = ring.tile([P, PACK, HALF], F32, name="pace_first", tag="first", bufs=1, align_bytes=64)
+            else:
+                tile = ring.tile([P, PACK, HALF], F32, name="rows", tag="rows", bufs=4)
+            rows = pace[KP * b : KP * (b + 1), HALF * h : HALF * (h + 1)]
+            nc.sync.dma_start(tile[:], rows.rearrange("(p t) j -> p t j", t=PACK))
+            pace_t[b, h] = tile
+
+        load_pace(0, 0)
+        load_pace(1, 0)
+        w3_raw = []
+        for a in range(2):
+            tile = ring.tile([P, PACK, HALF], F32, name="rows", tag="rows", bufs=4)
+            nc.sync.dma_start(tile[:], w3[KP * a : KP * (a + 1), :].rearrange("(p i) n -> p i n", i=PACK))
+            w3_raw.append(tile)
+        w2_raw = keep.tile([P, 2 * N], I32, name="w2_raw", align_bytes=64)
+        nc.sync.dma_start(
+            w2_raw[:].rearrange("p (a c) -> p a c", a=2),
+            w2_words.rearrange("a p c i -> p a (c i)").bitcast(I32),
+        )
+        for q in range(4):
+            nc.sync.dma_start(
+                w2_sc_raw[32 * q : 32 * q + 4, :].bitcast(I32).rearrange("p (a c) -> p a c", a=2),
+                w2_scales[:, 4 * q : 4 * q + 4, :].bitcast(I32).rearrange("a r c -> r a c"),
+            )
+        nc.sync.dma_start(place[:], offs2)
+        wgo_rows = wgo.rearrange("(q t) j -> q t j", t=PACK)
+        wgo_t = []
+
+        def load_wgo(h):
+            tile = keep.tile([P, PACK, HALF], F32, name="wgo%d" % h)
+            for q in (0, 2, 1, 3):
+                nc.sync.dma_start(tile[32 * q : 32 * (q + 1), :, :], wgo_rows[:, :, HALF * h : HALF * (h + 1)])
+            wgo_t.append(tile)
+
+        load_wgo(0)
+        load_pace(0, 1)
+        load_pace(1, 1)
+        load_wgo(1)
+        y = keep.tile([P, PACK, S], F32, name="y")
+        x0_rows = x0.rearrange("(p t) m -> p t m", t=PACK)
+        y_rows = out_0.rearrange("(p t) m -> p t m", t=PACK)
+        for t in range(PACK):
+            nc.sync.dma_start(y[:, t, :], x0_rows[:, t, :])
+
+        w1 = keep.tile([P, 2 * 2 * H], U8, name="w1", align_bytes=64)
+        nc.vector.tensor_copy(
+            w1[:].rearrange("p (g t m e) -> p g t m e", t=PACK, m=P, e=2),
+            w1_raw[:].rearrange("p (g m t e) -> p g t m e", t=PACK, m=P, e=2),
+        )
+        w1_sc = keep.tile([P, 2 * H], U8, name="w1_sc", align_bytes=64)
+        nc.vector.tensor_copy(
+            w1_sc[:].rearrange("p (g t m) -> p g t m", t=PACK, m=P),
+            w1_sc_raw[:].rearrange("p (g m t) -> p g t m", t=PACK, m=P),
+        )
+
+        v = {}
+        for a in range(2):
+            for h in range(2):
+                tile = keep.tile([P, HALF], U32, name="v%d%d" % (a, h), align_bytes=64)
+                nc.vector.tensor_copy(
+                    tile[:], tab[a][:].bitcast(U32).indirect(pick[:, LIST_COLS * h : LIST_COLS * (h + 1)])
+                )
+                v[a, h] = tile
+
+        def v_scales(a, h):
+            return v_sc[:, S * a + HALF * h : S * a + HALF * (h + 1)]
+
+        h_codes = {}
+        h_sc = {}
+
+        def hidden(b, h):
+            g = ring.tile([P, PACK, HALF], F32, name="g", tag="g", bufs=3)
+            for t in range(PACK):
+                acc = psum.tile([P, HALF], F32, name="acc", tag="acc")
+                for a in range(2):
+                    col = H * a + KP * b + P * t
+                    nc.tensor.matmul_mx(
+                        out=acc[:],
+                        lhsT=w1[:, 2 * col : 2 * (col + P)].bitcast(E2M1),
+                        lhsT_scale=w1_sc[:, col : col + P],
+                        rhs=v[a, h][:].bitcast(E4M3),
+                        rhs_scale=v_scales(a, h),
+                        start=(a == 0),
+                        stop=(a == 1),
+                    )
+                nc.scalar.activation(g[:, t, :], acc[:], ACT.Gelu_apprx_tanh)
+            hb = ring.tile([P, PACK * HALF], BF16, name="rounded", tag="rounded", bufs=4, align_bytes=64)
+            nc.vector.tensor_tensor(
+                hb[:].rearrange("p (c i t) -> p c t i", i=2, t=PACK),
+                g[:].rearrange("p t (c i) -> p c t i", i=2),
+                pace_t[b, h][:].rearrange("p t (c i) -> p c t i", i=2),
+                ALU.mult,
+            )
+            codes = keep.tile([P, HALF], U32, name="h_codes%d%d" % (b, h), align_bytes=64)
+            scales = keep.tile([P, HALF], U8, name="h_sc%d%d" % (b, h), align_bytes=64)
+            nc.vector.quantize_mx(out=codes[:].bitcast(E4M3), scales=scales[:], in_=hb[:])
+            h_codes[b, h] = codes
+            h_sc[b, h] = scales
+
+        hidden(0, 0)
+        hidden(1, 0)
+
+        w3_codes = []
+        w3_sc = []
+        for a in range(2):
+            wb = ring.tile([P, PACK * HALF], BF16, name="rounded", tag="rounded", bufs=4, align_bytes=64)
+            nc.scalar.copy(
+                wb[:].rearrange("p (t m i) -> p m t i", t=PACK, i=PACK),
+                w3_raw[a][:].rearrange("p i (m t) -> p m t i", t=PACK),
+            )
+            codes = keep.tile([P, N], U32, name="w3_codes%d" % a, align_bytes=64)
+            scales = keep.tile([P, N], U8, name="w3_sc%d" % a, align_bytes=64)
+            nc.vector.quantize_mx(out=codes[:].bitcast(E4M3), scales=scales[:], in_=wb[:])
+            w3_codes.append(codes)
+            w3_sc.append(scales)
+
+        w2 = keep.tile([P, 2 * N], I32, name="w2", align_bytes=64)
+        nc.vector.tensor_copy(
+            w2[:].rearrange("p (a t c i) -> p a c t i", a=2, t=PACK, i=4),
+            w2_raw[:].rearrange("p (a c i t) -> p a c t i", a=2, t=PACK, i=4),
+        )
+        w2_sc = keep.tile([P, 2 * N], U8, name="w2_sc", align_bytes=64)
+        nc.vector.tensor_copy(
+            w2_sc[:].rearrange("p (a t m) -> p a t m", t=PACK, m=P),
+            w2_sc_raw[:].rearrange("p (a m t) -> p a t m", t=PACK, m=P),
+        )
+
+        pages = [keep.tile([P, S], F32, name="page%d" % t) for t in range(PACK)]
+
+        def correct(t, h):
+            gate = psum.tile([P, HALF], F32, name="acc", tag="acc")
+            for a in range(2):
+                nc.tensor.matmul_mx(
+                    out=gate[:],
+                    lhsT=w3_codes[a][:, P * t : P * (t + 1)].bitcast(E4M3),
+                    lhsT_scale=w3_sc[a][:, P * t : P * (t + 1)],
+                    rhs=v[a, h][:].bitcast(E4M3),
+                    rhs_scale=v_scales(a, h),
+                    start=(a == 0),
+                    stop=(a == 1),
+                )
+            th = ring.tile([P, HALF], F32, name="th", tag="th", bufs=3)
+            nc.scalar.activation(th[:], gate[:], ACT.Tanh, scale=0.5)
+            acc = psum.tile([P, HALF], F32, name="acc", tag="acc")
+            for b in range(2):
+                col = N * b + P * t
+                nc.tensor.matmul_mx(
+                    out=acc[:],
+                    lhsT=w2[:, col : col + P].bitcast(E4M3),
+                    lhsT_scale=w2_sc[:, col : col + P],
+                    rhs=h_codes[b, h][:].bitcast(E4M3),
+                    rhs_scale=h_sc[b, h][:],
+                    start=(b == 0),
+                    stop=(b == 1),
+                )
+            f2 = ring.tile([P, HALF], F32, name="f2", tag="f2", bufs=3)
+            nc.vector.scalar_tensor_tensor(f2[:], th[:], 1.0, acc[:], ALU.add, ALU.mult)
+            nc.vector.tensor_tensor(
+                pages[t][:].indirect(place[:, LIST_COLS * h : LIST_COLS * (h + 1)]),
+                f2[:],
+                wgo_t[h][:, t, :],
+                ALU.mult,
+            )
+
+        def add_x0(t, cols):
+            nc.vector.scalar_tensor_tensor(y[:, t, cols], pages[t][:, cols], 0.5, y[:, t, cols], ALU.mult, ALU.add)
+
+        for t in range(PACK):
+            correct(t, 0)
+        hidden(0, 1)
+        hidden(1, 1)
+        for t in range(PACK):
+            correct(t, 1)
+            if t < PACK - 1:
+                add_x0(t, slice(0, S))
+                nc.sync.dma_start(y_rows[:, t, :], y[:, t, :])
+
+        y_codes = keep.tile([P, S], U32, name="y_codes", align_bytes=64)
+        y_sc = keep.tile([P, S], U8, name="y_sc", align_bytes=64)
+        code_rows = out_1[0].rearrange("p m t -> p (m t)").bitcast(I32)
+        last = PACK - 1
+        quarter = S // 4
+        for c in range(4):
+            add_x0(last, slice(quarter * c, quarter * (c + 1)))
+        for u in range(2):
+            cols = slice(HALF * u, HALF * (u + 1))
+            nc.sync.dma_start(y_rows[:, last, cols], y[:, last, cols])
+            yb = ring.tile([P, PACK * HALF], BF16, name="rounded", tag="rounded", bufs=4, align_bytes=64)
+            for w in range(2):
+                c = 2 * u + w
+                mcols = slice(quarter * c, quarter * (c + 1))
+                dst = yb[:, PACK * quarter * w : PACK * quarter * (w + 1)]
+                dst_v = dst.rearrange("p (c i t) -> p c t i", i=2, t=PACK)
+                src_v = y[:, :, mcols].rearrange("p t (c i) -> p c t i", i=2)
+                if w == 0:
+                    nc.scalar.copy(dst_v, src_v)
+                else:
+                    nc.vector.tensor_copy(dst_v, src_v)
+                nc.vector.quantize_mx(out=y_codes[:, mcols].bitcast(E4M3), scales=y_sc[:, mcols], in_=dst)
+            nc.sync.dma_start(code_rows[:, cols], y_codes[:, cols].bitcast(I32))
+        for q in range(4):
+            queue = nc.scalar if q % 2 else nc.sync
+            queue.dma_start(out_2[0, 4 * q : 4 * q + 4, :].bitcast(I32), y_sc[32 * q : 32 * q + 4, :].bitcast(I32))

@@ -31,6 +31,7 @@ def tile_list_transcript_corrections_kernel(
     with ExitStack() as ctx:
         lists = ctx.enter_context(tc.tile_pool(name="lists", bufs=1))
         keep = ctx.enter_context(tc.tile_pool(name="keep", bufs=1))
+        stage = ctx.enter_context(tc.tile_pool(name="stage", bufs=1))
         ring = ctx.enter_context(tc.tile_pool(name="ring", bufs=1))
         psum = ctx.enter_context(tc.psum_pool(name="psum", bufs=8))
 
@@ -42,120 +43,124 @@ def tile_list_transcript_corrections_kernel(
         warm_out = keep.tile([P, 8], F32, name="warm_out")
         nc.scalar.activation(warm_out[:], warm[:], ACT.Gelu_apprx_tanh)
 
-        tab_sc = ring.tile([P, T], U8, name="tab_sc", tag="first", bufs=1, align_bytes=64)
-        w1_sc_raw = keep.tile([P, 2 * H], U8, name="w1_sc_raw", align_bytes=64)
-        w2_sc_raw = keep.tile([P, 2 * N], U8, name="w2_sc_raw", align_bytes=64)
-        v_sc = keep.tile([P, 2 * S], U8, name="v_sc", align_bytes=64)
-        nc.vector.memset(w1_sc_raw[:].bitcast(I32), 0)
-        nc.vector.memset(tab_sc[32:64, :].bitcast(I32), 0)
-        nc.vector.memset(tab_sc[64:128, :].bitcast(I32), 0)
-        nc.vector.memset(v_sc[:].bitcast(I32), 0)
-        nc.vector.memset(w2_sc_raw[:].bitcast(I32), 0)
+        KB = 1024
+
+        def staged(shape, dtype, name, at):
+            return stage.tile(shape, dtype, name=name, align_bytes=64, offset=at * KB)
+
+        tab_sc = staged([P, 2 * T], U8, "tab_sc", 48)
+        w1_sc_raw = staged([P, 2 * H], U8, "w1_sc_raw", 40)
+        w1_raw = staged([P, 2 * 2 * H], U8, "w1_raw", 30)
+        nc.vector.memset(tab_sc[:].bitcast(I32), 0)
+        nc.gpsimd.memset(w1_sc_raw[:].bitcast(I32), 0)
+
+        def load_scale_rows(queue, tile, rows):
+            for q in range(4):
+                queue.dma_start(
+                    tile[32 * q : 32 * q + 4, :].bitcast(I32).rearrange("p (a c) -> p a c", a=2),
+                    rows[:, 4 * q : 4 * q + 4, :].bitcast(I32).rearrange("a r c -> r a c"),
+                )
+
+        def load_table(a, at):
+            words = staged([P, T], I32, "tab%d" % a, at)
+            nc.sync.dma_start(words[:], tab_words[a].rearrange("p t i -> p (t i)").bitcast(I32))
+            return words
 
         nc.sync.dma_start(pick[:], offs)
-        nc.sync.dma_start(tab_sc[0:32, :].bitcast(I32), tab_scales.rearrange("a q t -> (a q) t").bitcast(I32))
-        w1_raw = keep.tile([P, 2 * 2 * H], U8, name="w1_raw", align_bytes=64)
         nc.sync.dma_start(
             w1_raw[:].bitcast(I32).rearrange("p (a c) -> p a c", a=2),
             w1_words.bitcast(I32).rearrange("a p c -> p a c"),
         )
-        for q in range(4):
-            nc.gpsimd.dma_start(
-                w1_sc_raw[32 * q : 32 * q + 4, :].bitcast(I32).rearrange("p (a c) -> p a c", a=2),
-                w1_scales[:, 4 * q : 4 * q + 4, :].bitcast(I32).rearrange("a r c -> r a c"),
-            )
-        tab = []
-        for a in range(2):
-            words = keep.tile([P, T], I32, name="tab%d" % a, align_bytes=64)
-            nc.sync.dma_start(words[:], tab_words[a].rearrange("p t i -> p (t i)").bitcast(I32))
-            tab.append(words)
-
-        picked_sc = keep.tile([P, S], U8, name="picked_sc", align_bytes=64)
-        nc.vector.tensor_copy(picked_sc[:], tab_sc[:].indirect(pick[:]))
-        for a in range(2):
-            for q in range(4):
-                row = 16 * a + 4 * q
-                (nc.gpsimd if a else nc.scalar).dma_start(
-                    v_sc[32 * q : 32 * q + 4, S * a : S * (a + 1)].bitcast(I32),
-                    picked_sc[row : row + 4, :].bitcast(I32),
-                )
-
-        pace_t = {}
-
-        def load_pace(b, h):
-            if (b, h) == (0, 0):
-                tile = ring.tile([P, PACK, HALF], F32, name="pace_first", tag="first", bufs=1, align_bytes=64)
-            else:
-                tile = ring.tile([P, PACK, HALF], F32, name="rows", tag="rows", bufs=4)
-            rows = pace[KP * b : KP * (b + 1), HALF * h : HALF * (h + 1)]
-            nc.sync.dma_start(tile[:], rows.rearrange("(p t) j -> p t j", t=PACK))
-            pace_t[b, h] = tile
-
-        load_pace(0, 0)
-        load_pace(1, 0)
-        w3_raw = []
-        for a in range(2):
-            tile = ring.tile([P, PACK, HALF], F32, name="rows", tag="rows", bufs=4)
-            nc.sync.dma_start(tile[:], w3[KP * a : KP * (a + 1), :].rearrange("(p i) n -> p i n", i=PACK))
-            w3_raw.append(tile)
-        w2_raw = keep.tile([P, 2 * N], I32, name="w2_raw", align_bytes=64)
-        nc.sync.dma_start(
-            w2_raw[:].rearrange("p (a c) -> p a c", a=2),
-            w2_words.rearrange("a p c i -> p a (c i)").bitcast(I32),
-        )
-        for q in range(4):
-            nc.sync.dma_start(
-                w2_sc_raw[32 * q : 32 * q + 4, :].bitcast(I32).rearrange("p (a c) -> p a c", a=2),
-                w2_scales[:, 4 * q : 4 * q + 4, :].bitcast(I32).rearrange("a r c -> r a c"),
-            )
+        tab = [load_table(0, 0)]
         nc.sync.dma_start(place[:], offs2)
-        wgo_rows = wgo.rearrange("(q t) j -> q t j", t=PACK)
-        wgo_t = []
-
-        def load_wgo(h):
-            tile = keep.tile([P, PACK, HALF], F32, name="wgo%d" % h)
-            for q in (0, 2, 1, 3):
-                nc.sync.dma_start(tile[32 * q : 32 * (q + 1), :, :], wgo_rows[:, :, HALF * h : HALF * (h + 1)])
-            wgo_t.append(tile)
-
-        load_wgo(0)
-        load_pace(0, 1)
-        load_pace(1, 1)
-        load_wgo(1)
-        y = keep.tile([P, PACK, S], F32, name="y")
-        x0_rows = x0.rearrange("(p t) m -> p t m", t=PACK)
-        y_rows = out_0.rearrange("(p t) m -> p t m", t=PACK)
-        for t in range(PACK):
-            nc.sync.dma_start(y[:, t, :], x0_rows[:, t, :])
+        load_scale_rows(nc.scalar, w1_sc_raw, w1_scales)
+        load_scale_rows(nc.sync, tab_sc, tab_scales)
 
         w1 = keep.tile([P, 2 * 2 * H], U8, name="w1", align_bytes=64)
         nc.vector.tensor_copy(
             w1[:].rearrange("p (g t m e) -> p g t m e", t=PACK, m=P, e=2),
             w1_raw[:].rearrange("p (g m t e) -> p g t m e", t=PACK, m=P, e=2),
         )
+        tab.append(load_table(1, 16))
         w1_sc = keep.tile([P, 2 * H], U8, name="w1_sc", align_bytes=64)
         nc.vector.tensor_copy(
             w1_sc[:].rearrange("p (g t m) -> p g t m", t=PACK, m=P),
             w1_sc_raw[:].rearrange("p (g m t) -> p g t m", t=PACK, m=P),
         )
 
+        pace_t = {}
+
+        def load_pace(b, h, at):
+            tile = staged([P, PACK, HALF], F32, "pace%d%d" % (b, h), at)
+            rows = pace[KP * b : KP * (b + 1), HALF * h : HALF * (h + 1)]
+            nc.sync.dma_start(tile[:], rows.rearrange("(p t) j -> p t j", t=PACK))
+            pace_t[b, h] = tile
+
+        def load_w3(a, at):
+            tile = staged([P, PACK, HALF], F32, "w3_raw%d" % a, at)
+            nc.sync.dma_start(tile[:], w3[KP * a : KP * (a + 1), :].rearrange("(p i) n -> p i n", i=PACK))
+            return tile
+
+        wgo_rows = wgo.rearrange("(q t) j -> q t j", t=PACK)
+        wgo_t = []
+
+        def load_wgo(h, at):
+            tile = staged([P, PACK, HALF], F32, "wgo%d" % h, at)
+            for q in (0, 2, 1, 3):
+                nc.sync.dma_start(tile[32 * q : 32 * (q + 1), :, :], wgo_rows[:, :, HALF * h : HALF * (h + 1)])
+            wgo_t.append(tile)
+
+        load_pace(0, 0, 32)
+
         v = {}
-        for a in range(2):
-            for h in range(2):
-                tile = keep.tile([P, HALF], U32, name="v%d%d" % (a, h), align_bytes=64)
-                nc.vector.tensor_copy(
-                    tile[:], tab[a][:].bitcast(U32).indirect(pick[:, LIST_COLS * h : LIST_COLS * (h + 1)])
-                )
-                v[a, h] = tile
+        v_sc = {}
+
+        def gather_words(a, h):
+            tile = keep.tile([P, HALF], U32, name="v%d%d" % (a, h), align_bytes=64)
+            nc.vector.tensor_copy(
+                tile[:], tab[a][:].bitcast(U32).indirect(pick[:, LIST_COLS * h : LIST_COLS * (h + 1)])
+            )
+            v[a, h] = tile
+
+        def gather_scales(a, h):
+            tile = keep.tile([P, HALF], U8, name="v_sc%d%d" % (a, h), align_bytes=64)
+            nc.vector.tensor_copy(
+                tile[:], tab_sc[:, T * a : T * (a + 1)].indirect(pick[:, LIST_COLS * h : LIST_COLS * (h + 1)])
+            )
+            v_sc[a, h] = tile
+
+        gather_words(0, 0)
+        gather_words(0, 1)
+        w3_raw = [load_w3(0, 40), load_w3(1, 0)]
+        gather_scales(0, 0)
+        gather_scales(1, 0)
+        load_pace(1, 0, 8)
+        gather_words(1, 0)
+        gather_scales(0, 1)
+        gather_scales(1, 1)
+        gather_words(1, 1)
+        w2_raw = staged([P, 2 * N], I32, "w2_raw", 48)
+        nc.sync.dma_start(
+            w2_raw[:].rearrange("p (a c) -> p a c", a=2),
+            w2_words.rearrange("a p c i -> p a (c i)").bitcast(I32),
+        )
+        w2_sc_raw = staged([P, N], U8, "w2_sc_raw", 52)
+        nc.gpsimd.memset(w2_sc_raw[:].bitcast(I32), 0)
+        for q in range(4):
+            nc.sync.dma_start(
+                w2_sc_raw[32 * q : 32 * q + 8, :].bitcast(I32), w2_scales[:, 4 * q : 4 * q + 4, :].bitcast(I32)
+            )
+        load_pace(0, 1, 24)
+        load_wgo(0, 16)
 
         def v_scales(a, h):
-            return v_sc[:, S * a + HALF * h : S * a + HALF * (h + 1)]
+            return v_sc[a, h][:]
 
         h_codes = {}
         h_sc = {}
 
         def hidden(b, h):
-            g = ring.tile([P, PACK, HALF], F32, name="g", tag="g", bufs=3)
+            g = ring.tile([P, PACK, HALF], F32, name="g", tag="g", bufs=4)
             for t in range(PACK):
                 acc = psum.tile([P, HALF], F32, name="acc", tag="acc")
                 for a in range(2):
@@ -184,7 +189,7 @@ def tile_list_transcript_corrections_kernel(
             h_sc[b, h] = scales
 
         hidden(0, 0)
-        hidden(1, 0)
+        load_pace(1, 1, 32)
 
         w3_codes = []
         w3_sc = []
@@ -200,15 +205,25 @@ def tile_list_transcript_corrections_kernel(
             w3_codes.append(codes)
             w3_sc.append(scales)
 
+        hidden(1, 0)
+        load_wgo(1, 40)
+        x0_rows = x0.rearrange("(p t) m -> p t m", t=PACK)
+        y_rows = out_0.rearrange("(p t) m -> p t m", t=PACK)
+        y = []
+        for u in range(2):
+            tile = staged([P, PACK, HALF], F32, "y%d" % u, 8 * u)
+            nc.sync.dma_start(tile[:], x0_rows[:, :, HALF * u : HALF * (u + 1)])
+            y.append(tile)
+
         w2 = keep.tile([P, 2 * N], I32, name="w2", align_bytes=64)
         nc.vector.tensor_copy(
             w2[:].rearrange("p (a t c i) -> p a c t i", a=2, t=PACK, i=4),
             w2_raw[:].rearrange("p (a c i t) -> p a c t i", a=2, t=PACK, i=4),
         )
-        w2_sc = keep.tile([P, 2 * N], U8, name="w2_sc", align_bytes=64)
+        w2_sc = keep.tile([P, N], U8, name="w2_sc", align_bytes=64)
         nc.vector.tensor_copy(
-            w2_sc[:].rearrange("p (a t m) -> p a t m", t=PACK, m=P),
-            w2_sc_raw[:].rearrange("p (a m t) -> p a t m", t=PACK, m=P),
+            w2_sc[:].rearrange("p (t m) -> p t m", t=PACK),
+            w2_sc_raw[:].rearrange("p (m t) -> p t m", t=PACK),
         )
 
         pages = [keep.tile([P, S], F32, name="page%d" % t) for t in range(PACK)]
@@ -227,57 +242,67 @@ def tile_list_transcript_corrections_kernel(
                 )
             th = ring.tile([P, HALF], F32, name="th", tag="th", bufs=3)
             nc.scalar.activation(th[:], gate[:], ACT.Tanh, scale=0.5)
+            nc.scalar.activation(th[:], th[:], ACT.Copy, scale=0.5, bias=0.5)
+            weight = wgo_t[h][:, t, :]
+            nc.gpsimd.tensor_tensor(weight, th[:], weight, ALU.mult)
             acc = psum.tile([P, HALF], F32, name="acc", tag="acc")
             for b in range(2):
                 col = N * b + P * t
                 nc.tensor.matmul_mx(
                     out=acc[:],
                     lhsT=w2[:, col : col + P].bitcast(E4M3),
-                    lhsT_scale=w2_sc[:, col : col + P],
+                    lhsT_scale=w2_sc[4 * b :, P * t : P * (t + 1)],
                     rhs=h_codes[b, h][:].bitcast(E4M3),
                     rhs_scale=h_sc[b, h][:],
                     start=(b == 0),
                     stop=(b == 1),
                 )
-            f2 = ring.tile([P, HALF], F32, name="f2", tag="f2", bufs=3)
-            nc.vector.scalar_tensor_tensor(f2[:], th[:], 1.0, acc[:], ALU.add, ALU.mult)
-            nc.vector.tensor_tensor(
-                pages[t][:].indirect(place[:, LIST_COLS * h : LIST_COLS * (h + 1)]),
-                f2[:],
-                wgo_t[h][:, t, :],
-                ALU.mult,
-            )
+            if h == 0:
+                f = ring.tile([P, HALF], F32, name="f", tag="f", bufs=3)
+                nc.vector.tensor_tensor(f[:], weight, acc[:], ALU.mult)
+            else:
+                f = ring.tile([P, HALF], F32, name="f_late", tag="f_late", bufs=4)
+                nc.scalar.copy(f[:], acc[:])
+                nc.gpsimd.tensor_tensor(f[:], f[:], weight, ALU.mult)
+            return f
 
-        def add_x0(t, cols):
-            nc.vector.scalar_tensor_tensor(y[:, t, cols], pages[t][:, cols], 0.5, y[:, t, cols], ALU.mult, ALU.add)
+        def put(t, h, f):
+            nc.vector.tensor_copy(pages[t][:].indirect(place[:, LIST_COLS * h : LIST_COLS * (h + 1)]), f[:])
 
-        for t in range(PACK):
-            correct(t, 0)
+        def add_x0(engine, t, u):
+            cols = slice(HALF * u, HALF * (u + 1))
+            engine.tensor_tensor(y[u][:, t, :], pages[t][:, cols], y[u][:, t, :], ALU.add)
+            nc.sync.dma_start(y_rows[:, t, cols], y[u][:, t, :])
+
+        units = [(t, h) for h in range(2) for t in range(PACK)]
         hidden(0, 1)
-        hidden(1, 1)
-        for t in range(PACK):
-            correct(t, 1)
-            if t < PACK - 1:
-                add_x0(t, slice(0, S))
-                nc.sync.dma_start(y_rows[:, t, :], y[:, t, :])
+        made = [correct(*units[0])]
+        for n, (t, h) in enumerate(units):
+            if n == 0:
+                hidden(1, 1)
+            if n + 1 < len(units):
+                made.append(correct(*units[n + 1]))
+            put(t, h, made[n])
+            if h == 1 and t < PACK - 1:
+                for u in range(2):
+                    add_x0(nc.gpsimd, t, u)
 
         y_codes = keep.tile([P, S], U32, name="y_codes", align_bytes=64)
         y_sc = keep.tile([P, S], U8, name="y_sc", align_bytes=64)
         code_rows = out_1[0].rearrange("p m t -> p (m t)").bitcast(I32)
         last = PACK - 1
         quarter = S // 4
-        for c in range(4):
-            add_x0(last, slice(quarter * c, quarter * (c + 1)))
+        for u in range(2):
+            add_x0(nc.vector, last, u)
         for u in range(2):
             cols = slice(HALF * u, HALF * (u + 1))
-            nc.sync.dma_start(y_rows[:, last, cols], y[:, last, cols])
             yb = ring.tile([P, PACK * HALF], BF16, name="rounded", tag="rounded", bufs=4, align_bytes=64)
             for w in range(2):
                 c = 2 * u + w
                 mcols = slice(quarter * c, quarter * (c + 1))
                 dst = yb[:, PACK * quarter * w : PACK * quarter * (w + 1)]
                 dst_v = dst.rearrange("p (c i t) -> p c t i", i=2, t=PACK)
-                src_v = y[:, :, mcols].rearrange("p t (c i) -> p c t i", i=2)
+                src_v = y[u][:, :, quarter * w : quarter * (w + 1)].rearrange("p t (c i) -> p c t i", i=2)
                 if w == 0:
                     nc.scalar.copy(dst_v, src_v)
                 else:

@@ -38,16 +38,15 @@ def tile_list_transcript_corrections_kernel(
         pick = lists.tile([P, S // 16], U16, name="pick")
         place = lists.tile([P, S // 16], U16, name="place")
 
-        warm = keep.tile([P, 8], F32, name="warm")
-        nc.gpsimd.memset(warm[:], 0.0)
-        warm_out = keep.tile([P, 8], F32, name="warm_out")
-        nc.scalar.activation(warm_out[:], warm[:], ACT.Gelu_apprx_tanh)
 
         KB = 1024
 
         def staged(shape, dtype, name, at):
             return stage.tile(shape, dtype, name=name, align_bytes=64, offset=at * KB)
 
+        warm = staged([P, 16], F32, "warm", 0)
+        nc.gpsimd.memset(warm[:], 0.0)
+        nc.scalar.activation(warm[:, 8:16], warm[:, 0:8], ACT.Gelu_apprx_tanh)
         tab_sc = staged([P, 2 * T], U8, "tab_sc", 48)
         w1_sc_raw = staged([P, 2 * H], U8, "w1_sc_raw", 40)
         w1_raw = staged([P, 2 * 2 * H], U8, "w1_raw", 30)
@@ -71,10 +70,10 @@ def tile_list_transcript_corrections_kernel(
             w1_raw[:].bitcast(I32).rearrange("p (a c) -> p a c", a=2),
             w1_words.bitcast(I32).rearrange("a p c -> p a c"),
         )
-        tab = [load_table(0, 0)]
         nc.sync.dma_start(place[:], offs2)
-        load_scale_rows(nc.scalar, w1_sc_raw, w1_scales)
         load_scale_rows(nc.sync, tab_sc, tab_scales)
+        tab = [load_table(0, 0)]
+        load_scale_rows(nc.scalar, w1_sc_raw, w1_scales)
 
         w1 = keep.tile([P, 2 * 2 * H], U8, name="w1", align_bytes=64)
         nc.vector.tensor_copy(
@@ -110,7 +109,7 @@ def tile_list_transcript_corrections_kernel(
                 nc.sync.dma_start(tile[32 * q : 32 * (q + 1), :, :], wgo_rows[:, :, HALF * h : HALF * (h + 1)])
             wgo_t.append(tile)
 
-        load_pace(0, 0, 32)
+        w3_raw = [load_w3(0, 32)]
 
         v = {}
         v_sc = {}
@@ -129,29 +128,18 @@ def tile_list_transcript_corrections_kernel(
             )
             v_sc[a, h] = tile
 
+        for h in range(2):
+            for a in range(2):
+                gather_scales(a, h)
+        load_pace(0, 0, 48)
         gather_words(0, 0)
         gather_words(0, 1)
-        w3_raw = [load_w3(0, 40), load_w3(1, 0)]
-        gather_scales(0, 0)
-        gather_scales(1, 0)
-        load_pace(1, 0, 8)
+        load_pace(1, 0, 0)
+        w3_raw.append(load_w3(1, 8))
         gather_words(1, 0)
-        gather_scales(0, 1)
-        gather_scales(1, 1)
         gather_words(1, 1)
-        w2_raw = staged([P, 2 * N], I32, "w2_raw", 48)
-        nc.sync.dma_start(
-            w2_raw[:].rearrange("p (a c) -> p a c", a=2),
-            w2_words.rearrange("a p c i -> p a (c i)").bitcast(I32),
-        )
-        w2_sc_raw = staged([P, N], U8, "w2_sc_raw", 52)
-        nc.gpsimd.memset(w2_sc_raw[:].bitcast(I32), 0)
-        for q in range(4):
-            nc.sync.dma_start(
-                w2_sc_raw[32 * q : 32 * q + 8, :].bitcast(I32), w2_scales[:, 4 * q : 4 * q + 4, :].bitcast(I32)
-            )
-        load_pace(0, 1, 24)
-        load_wgo(0, 16)
+        load_pace(0, 1, 16)
+        load_pace(1, 1, 24)
 
         def v_scales(a, h):
             return v_sc[a, h][:]
@@ -159,8 +147,12 @@ def tile_list_transcript_corrections_kernel(
         h_codes = {}
         h_sc = {}
 
-        def hidden(b, h):
-            g = ring.tile([P, PACK, HALF], F32, name="g", tag="g", bufs=4)
+        def hidden(b, h, pieces=1):
+            sums = []
+            if (b, h) == (1, 1):
+                g = staged([P, PACK, HALF], F32, "g_last", 8)
+            else:
+                g = ring.tile([P, PACK, HALF], F32, name="g", tag="g", bufs=3)
             for t in range(PACK):
                 acc = psum.tile([P, HALF], F32, name="acc", tag="acc")
                 for a in range(2):
@@ -174,28 +166,31 @@ def tile_list_transcript_corrections_kernel(
                         start=(a == 0),
                         stop=(a == 1),
                     )
-                nc.scalar.activation(g[:, t, :], acc[:], ACT.Gelu_apprx_tanh)
+                sums.append(acc)
             hb = ring.tile([P, PACK * HALF], BF16, name="rounded", tag="rounded", bufs=4, align_bytes=64)
-            nc.vector.tensor_tensor(
-                hb[:].rearrange("p (c i t) -> p c t i", i=2, t=PACK),
-                g[:].rearrange("p t (c i) -> p c t i", i=2),
-                pace_t[b, h][:].rearrange("p t (c i) -> p c t i", i=2),
-                ALU.mult,
-            )
+            width = HALF // pieces
+            for piece in range(pieces):
+                cols = slice(width * piece, width * (piece + 1))
+                for t in range(PACK):
+                    nc.scalar.activation(g[:, t, cols], sums[t][:, cols], ACT.Gelu_apprx_tanh)
+                nc.vector.tensor_tensor(
+                    hb[:, PACK * cols.start : PACK * cols.stop].rearrange("p (c i t) -> p c t i", i=2, t=PACK),
+                    g[:, :, cols].rearrange("p t (c i) -> p c t i", i=2),
+                    pace_t[b, h][:, :, cols].rearrange("p t (c i) -> p c t i", i=2),
+                    ALU.mult,
+                )
             codes = keep.tile([P, HALF], U32, name="h_codes%d%d" % (b, h), align_bytes=64)
             scales = keep.tile([P, HALF], U8, name="h_sc%d%d" % (b, h), align_bytes=64)
             nc.vector.quantize_mx(out=codes[:].bitcast(E4M3), scales=scales[:], in_=hb[:])
             h_codes[b, h] = codes
             h_sc[b, h] = scales
 
-        hidden(0, 0)
-        load_pace(1, 1, 32)
-
         w3_codes = []
         w3_sc = []
-        for a in range(2):
+
+        def quantise_w3(a, round_copy):
             wb = ring.tile([P, PACK * HALF], BF16, name="rounded", tag="rounded", bufs=4, align_bytes=64)
-            nc.scalar.copy(
+            round_copy(
                 wb[:].rearrange("p (t m i) -> p m t i", t=PACK, i=PACK),
                 w3_raw[a][:].rearrange("p i (m t) -> p m t i", t=PACK),
             )
@@ -205,15 +200,29 @@ def tile_list_transcript_corrections_kernel(
             w3_codes.append(codes)
             w3_sc.append(scales)
 
+        quantise_w3(0, nc.vector.tensor_copy)
+        w2_raw = staged([P, 2 * N], I32, "w2_raw", 32)
+        nc.sync.dma_start(
+            w2_raw[:].rearrange("p (a c) -> p a c", a=2),
+            w2_words.rearrange("a p c i -> p a (c i)").bitcast(I32),
+        )
+        w2_sc_raw = staged([P, N], U8, "w2_sc_raw", 36)
+        nc.gpsimd.memset(w2_sc_raw[:].bitcast(I32), 0)
+        for q in range(4):
+            nc.sync.dma_start(
+                w2_sc_raw[32 * q : 32 * q + 8, :].bitcast(I32), w2_scales[:, 4 * q : 4 * q + 4, :].bitcast(I32)
+            )
+
+
+        hidden(0, 0)
+        load_wgo(0, 48)
         hidden(1, 0)
-        load_wgo(1, 40)
+        load_wgo(1, 0)
+        hidden(0, 1)
+        quantise_w3(1, nc.scalar.copy)
+        hidden(1, 1)
         x0_rows = x0.rearrange("(p t) m -> p t m", t=PACK)
         y_rows = out_0.rearrange("(p t) m -> p t m", t=PACK)
-        y = []
-        for u in range(2):
-            tile = staged([P, PACK, HALF], F32, "y%d" % u, 8 * u)
-            nc.sync.dma_start(tile[:], x0_rows[:, :, HALF * u : HALF * (u + 1)])
-            y.append(tile)
 
         w2 = keep.tile([P, 2 * N], I32, name="w2", align_bytes=64)
         nc.vector.tensor_copy(
@@ -228,7 +237,7 @@ def tile_list_transcript_corrections_kernel(
 
         pages = [keep.tile([P, S], F32, name="page%d" % t) for t in range(PACK)]
 
-        def correct(t, h):
+        def gated_weight(n, t, h):
             gate = psum.tile([P, HALF], F32, name="acc", tag="acc")
             for a in range(2):
                 nc.tensor.matmul_mx(
@@ -240,11 +249,17 @@ def tile_list_transcript_corrections_kernel(
                     start=(a == 0),
                     stop=(a == 1),
                 )
-            th = ring.tile([P, HALF], F32, name="th", tag="th", bufs=3)
+            if n == 0:
+                th = keep.tile([P, HALF], F32, name="gate_first")
+            else:
+                th = staged([P, HALF], F32, "gate%d" % n, 24 + 2 * ((n - 1) % 4))
             nc.scalar.activation(th[:], gate[:], ACT.Tanh, scale=0.5)
             nc.scalar.activation(th[:], th[:], ACT.Copy, scale=0.5, bias=0.5)
             weight = wgo_t[h][:, t, :]
-            nc.gpsimd.tensor_tensor(weight, th[:], weight, ALU.mult)
+            (nc.gpsimd if n else nc.vector).tensor_tensor(weight, th[:], weight, ALU.mult)
+            return weight
+
+        def correct(t, h, weight):
             acc = psum.tile([P, HALF], F32, name="acc", tag="acc")
             for b in range(2):
                 col = N * b + P * t
@@ -275,17 +290,27 @@ def tile_list_transcript_corrections_kernel(
             nc.sync.dma_start(y_rows[:, t, cols], y[u][:, t, :])
 
         units = [(t, h) for h in range(2) for t in range(PACK)]
-        hidden(0, 1)
-        made = [correct(*units[0])]
-        for n, (t, h) in enumerate(units):
-            if n == 0:
-                hidden(1, 1)
+        y = []
+        made = {}
+
+        def make(n):
+            made[n] = correct(*units[n], gated_weight(n, *units[n]))
+
+        make(0)
+        put(*units[0], made[0])
+        make(1)
+        for n in range(1, len(units)):
             if n + 1 < len(units):
-                made.append(correct(*units[n + 1]))
-            put(t, h, made[n])
-            if h == 1 and t < PACK - 1:
-                for u in range(2):
-                    add_x0(nc.gpsimd, t, u)
+                make(n + 1)
+            put(*units[n], made[n])
+        for u in range(2):
+            tile = staged([P, PACK, HALF], F32, "y%d" % u, 44 + 8 * u)
+            nc.sync.dma_start(tile[:], x0_rows[:, :, HALF * u : HALF * (u + 1)])
+            y.append(tile)
+
+        for t in range(PACK - 1):
+            for u in range(2):
+                add_x0(nc.gpsimd, t, u)
 
         y_codes = keep.tile([P, S], U32, name="y_codes", align_bytes=64)
         y_sc = keep.tile([P, S], U8, name="y_sc", align_bytes=64)

@@ -18,9 +18,13 @@ ALU = mybir.AluOpType
 
 P = 128
 PACK = 4
-KP = P * PACK
+PASS = P * PACK
 HALF = 512
+QUARTER = S // 4
 LIST_COLS = HALF // 16
+KIB = 1024
+GATE_SLOTS = 3
+VECTOR_UNITS = 2
 
 
 def tile_list_transcript_corrections_kernel(
@@ -35,305 +39,286 @@ def tile_list_transcript_corrections_kernel(
         ring = ctx.enter_context(tc.tile_pool(name="ring", bufs=1))
         psum = ctx.enter_context(tc.psum_pool(name="psum", bufs=8))
 
+        def staged(shape, dtype, name, at_kib):
+            return stage.tile(shape, dtype, name=name, align_bytes=64, offset=at_kib * KIB)
+
+        def half_cols(u):
+            return slice(HALF * u, HALF * (u + 1))
+
+        def list_half(tile, u):
+            return tile[:, LIST_COLS * u : LIST_COLS * (u + 1)]
+
+        def rounded_tile():
+            return ring.tile([P, PACK * HALF], BF16, name="rounded", tag="rounded", bufs=4, align_bytes=64)
+
+        def quantise(rounded, name):
+            codes = keep.tile([P, HALF], U32, name=name + "_codes", align_bytes=64)
+            scales = keep.tile([P, HALF], U8, name=name + "_scales", align_bytes=64)
+            nc.vector.quantize_mx(out=codes[:].bitcast(E4M3), scales=scales[:], in_=rounded[:])
+            return codes, scales
+
+        def interleaved(rounded):
+            return rounded.rearrange("p (c i t) -> p c t i", i=2, t=PACK)
+
+        def by_slices(rows):
+            return rows.rearrange("p t (c i) -> p c t i", i=2)
+
+        def load_scale_rows(tile, rows):
+            for r in range(4):
+                nc.sync.dma_start(
+                    tile[r:P:32, :].bitcast(I32).rearrange("p (a c) -> p a c", a=2),
+                    rows[:, r:16:4, :].bitcast(I32).rearrange("a q c -> q a c"),
+                )
+
+        def load_table(a, at_kib):
+            words = staged([P, T], I32, "table%d" % a, at_kib)
+            nc.sync.dma_start(words[:], tab_words[a].rearrange("p t i -> p (t i)").bitcast(I32))
+            return words
+
+        def load_rows(rows, name, at_kib):
+            tile = staged([P, PACK, HALF], F32, name, at_kib)
+            nc.sync.dma_start(tile[:], rows.rearrange("(p t) c -> p t c", t=PACK))
+            return tile
+
+        def load_pace(b, u, at_kib):
+            return load_rows(pace[PASS * b : PASS * (b + 1), half_cols(u)], "pace%d%d" % (b, u), at_kib)
+
+        def load_w3(a, at_kib):
+            return load_rows(w3[PASS * a : PASS * (a + 1), :], "w3_raw%d" % a, at_kib)
+
+        wgo_rows = wgo.rearrange("(q t) j -> q t j", t=PACK)
+        weights = {}
+
+        def load_wgo(u, t0, count, at_kib):
+            tile = staged([P, count, HALF], F32, "wgo%d%d" % (u, t0), at_kib)
+            for q in (0, 2, 1, 3):
+                nc.sync.dma_start(tile[32 * q : 32 * (q + 1), :, :], wgo_rows[:, t0 : t0 + count, half_cols(u)])
+            for t in range(t0, t0 + count):
+                weights[t, u] = tile[:, t - t0, :]
+
         pick = lists.tile([P, S // 16], U16, name="pick")
         place = lists.tile([P, S // 16], U16, name="place")
 
-
-        KB = 1024
-
-        def staged(shape, dtype, name, at):
-            return stage.tile(shape, dtype, name=name, align_bytes=64, offset=at * KB)
-
-        warm = staged([P, 16], F32, "warm", 0)
-        nc.gpsimd.memset(warm[:], 0.0)
-        nc.scalar.activation(warm[:, 8:16], warm[:, 0:8], ACT.Gelu_apprx_tanh)
-        tab_sc = staged([P, 2 * T], U8, "tab_sc", 48)
-        w1_sc_raw = staged([P, 2 * H], U8, "w1_sc_raw", 40)
+        table_scales = staged([P, 2 * T], U8, "table_scales", 48)
+        w1_scales_raw = staged([P, 2 * H], U8, "w1_scales_raw", 40)
         w1_raw = staged([P, 2 * 2 * H], U8, "w1_raw", 30)
-        nc.vector.memset(tab_sc[:].bitcast(I32), 0)
-        nc.gpsimd.memset(w1_sc_raw[:].bitcast(I32), 0)
-
-        def load_scale_rows(queue, tile, rows):
-            for q in range(4):
-                queue.dma_start(
-                    tile[32 * q : 32 * q + 4, :].bitcast(I32).rearrange("p (a c) -> p a c", a=2),
-                    rows[:, 4 * q : 4 * q + 4, :].bitcast(I32).rearrange("a r c -> r a c"),
-                )
-
-        def load_table(a, at):
-            words = staged([P, T], I32, "tab%d" % a, at)
-            nc.sync.dma_start(words[:], tab_words[a].rearrange("p t i -> p (t i)").bitcast(I32))
-            return words
+        nc.vector.memset(table_scales[:].bitcast(I32), 0)
+        nc.gpsimd.memset(w1_scales_raw[:].bitcast(I32), 0)
 
         nc.sync.dma_start(pick[:], offs)
         nc.sync.dma_start(
             w1_raw[:].bitcast(I32).rearrange("p (a c) -> p a c", a=2),
             w1_words.bitcast(I32).rearrange("a p c -> p a c"),
         )
+        table = [load_table(0, 0)]
         nc.sync.dma_start(place[:], offs2)
-        load_scale_rows(nc.sync, tab_sc, tab_scales)
-        tab = [load_table(0, 0)]
-        load_scale_rows(nc.scalar, w1_sc_raw, w1_scales)
+        load_scale_rows(w1_scales_raw, w1_scales)
+        load_scale_rows(table_scales, tab_scales)
 
         w1 = keep.tile([P, 2 * 2 * H], U8, name="w1", align_bytes=64)
         nc.vector.tensor_copy(
             w1[:].rearrange("p (g t m e) -> p g t m e", t=PACK, m=P, e=2),
             w1_raw[:].rearrange("p (g m t e) -> p g t m e", t=PACK, m=P, e=2),
         )
-        tab.append(load_table(1, 16))
-        w1_sc = keep.tile([P, 2 * H], U8, name="w1_sc", align_bytes=64)
+        table.append(load_table(1, 16))
+        w3_raw = [load_w3(0, 32)]
+        w1_dealt_scales = keep.tile([P, 2 * H], U8, name="w1_dealt_scales", align_bytes=64)
         nc.vector.tensor_copy(
-            w1_sc[:].rearrange("p (g t m) -> p g t m", t=PACK, m=P),
-            w1_sc_raw[:].rearrange("p (g m t) -> p g t m", t=PACK, m=P),
+            w1_dealt_scales[:].rearrange("p (g t m) -> p g t m", t=PACK, m=P),
+            w1_scales_raw[:].rearrange("p (g m t) -> p g t m", t=PACK, m=P),
         )
 
-        pace_t = {}
+        picked = {}
+        picked_scales = {}
 
-        def load_pace(b, h, at):
-            tile = staged([P, PACK, HALF], F32, "pace%d%d" % (b, h), at)
-            rows = pace[KP * b : KP * (b + 1), HALF * h : HALF * (h + 1)]
-            nc.sync.dma_start(tile[:], rows.rearrange("(p t) j -> p t j", t=PACK))
-            pace_t[b, h] = tile
+        def gather_words(a, u):
+            tile = keep.tile([P, HALF], U32, name="picked%d%d" % (a, u), align_bytes=64)
+            nc.vector.tensor_copy(tile[:], table[a][:].bitcast(U32).indirect(list_half(pick, u)))
+            picked[a, u] = tile
 
-        def load_w3(a, at):
-            tile = staged([P, PACK, HALF], F32, "w3_raw%d" % a, at)
-            nc.sync.dma_start(tile[:], w3[KP * a : KP * (a + 1), :].rearrange("(p i) n -> p i n", i=PACK))
-            return tile
+        def gather_scales(a, u):
+            tile = keep.tile([P, HALF], U8, name="picked_scales%d%d" % (a, u), align_bytes=64)
+            nc.vector.tensor_copy(tile[:], table_scales[:, T * a : T * (a + 1)].indirect(list_half(pick, u)))
+            picked_scales[a, u] = tile
 
-        wgo_rows = wgo.rearrange("(q t) j -> q t j", t=PACK)
-        wgo_t = []
-
-        def load_wgo(h, at):
-            tile = staged([P, PACK, HALF], F32, "wgo%d" % h, at)
-            for q in (0, 2, 1, 3):
-                nc.sync.dma_start(tile[32 * q : 32 * (q + 1), :, :], wgo_rows[:, :, HALF * h : HALF * (h + 1)])
-            wgo_t.append(tile)
-
-        w3_raw = [load_w3(0, 32)]
-
-        v = {}
-        v_sc = {}
-
-        def gather_words(a, h):
-            tile = keep.tile([P, HALF], U32, name="v%d%d" % (a, h), align_bytes=64)
-            nc.vector.tensor_copy(
-                tile[:], tab[a][:].bitcast(U32).indirect(pick[:, LIST_COLS * h : LIST_COLS * (h + 1)])
-            )
-            v[a, h] = tile
-
-        def gather_scales(a, h):
-            tile = keep.tile([P, HALF], U8, name="v_sc%d%d" % (a, h), align_bytes=64)
-            nc.vector.tensor_copy(
-                tile[:], tab_sc[:, T * a : T * (a + 1)].indirect(pick[:, LIST_COLS * h : LIST_COLS * (h + 1)])
-            )
-            v_sc[a, h] = tile
-
-        for h in range(2):
+        paces = {}
+        for u in range(2):
+            gather_words(0, u)
+        for u in range(2):
             for a in range(2):
-                gather_scales(a, h)
-        load_pace(0, 0, 48)
-        gather_words(0, 0)
-        gather_words(0, 1)
-        load_pace(1, 0, 0)
-        w3_raw.append(load_w3(1, 8))
-        gather_words(1, 0)
-        gather_words(1, 1)
-        load_pace(0, 1, 16)
-        load_pace(1, 1, 24)
+                gather_scales(a, u)
+        paces[0, 0] = load_pace(0, 0, 8)
+        paces[1, 0] = load_pace(1, 0, 0)
+        paces[0, 1] = load_pace(0, 1, 48)
+        for u in range(2):
+            gather_words(1, u)
+        w3_raw.append(load_w3(1, 16))
+        paces[1, 1] = load_pace(1, 1, 24)
 
-        def v_scales(a, h):
-            return v_sc[a, h][:]
-
-        h_codes = {}
-        h_sc = {}
-
-        def hidden(b, h, pieces=1):
-            sums = []
-            if (b, h) == (1, 1):
-                g = staged([P, PACK, HALF], F32, "g_last", 8)
-            else:
-                g = ring.tile([P, PACK, HALF], F32, name="g", tag="g", bufs=3)
-            for t in range(PACK):
-                acc = psum.tile([P, HALF], F32, name="acc", tag="acc")
-                for a in range(2):
-                    col = H * a + KP * b + P * t
-                    nc.tensor.matmul_mx(
-                        out=acc[:],
-                        lhsT=w1[:, 2 * col : 2 * (col + P)].bitcast(E2M1),
-                        lhsT_scale=w1_sc[:, col : col + P],
-                        rhs=v[a, h][:].bitcast(E4M3),
-                        rhs_scale=v_scales(a, h),
-                        start=(a == 0),
-                        stop=(a == 1),
-                    )
-                sums.append(acc)
-            hb = ring.tile([P, PACK * HALF], BF16, name="rounded", tag="rounded", bufs=4, align_bytes=64)
-            width = HALF // pieces
-            for piece in range(pieces):
-                cols = slice(width * piece, width * (piece + 1))
-                for t in range(PACK):
-                    nc.scalar.activation(g[:, t, cols], sums[t][:, cols], ACT.Gelu_apprx_tanh)
-                nc.vector.tensor_tensor(
-                    hb[:, PACK * cols.start : PACK * cols.stop].rearrange("p (c i t) -> p c t i", i=2, t=PACK),
-                    g[:, :, cols].rearrange("p t (c i) -> p c t i", i=2),
-                    pace_t[b, h][:, :, cols].rearrange("p t (c i) -> p c t i", i=2),
-                    ALU.mult,
+        def product(stationary, moving):
+            acc = psum.tile([P, HALF], F32, name="acc", tag="acc")
+            for a in range(2):
+                nc.tensor.matmul_mx(
+                    out=acc[:],
+                    lhsT=stationary[a][0],
+                    lhsT_scale=stationary[a][1],
+                    rhs=moving[a][0][:].bitcast(E4M3),
+                    rhs_scale=moving[a][1][:],
+                    start=(a == 0),
+                    stop=(a == 1),
                 )
-            codes = keep.tile([P, HALF], U32, name="h_codes%d%d" % (b, h), align_bytes=64)
-            scales = keep.tile([P, HALF], U8, name="h_sc%d%d" % (b, h), align_bytes=64)
-            nc.vector.quantize_mx(out=codes[:].bitcast(E4M3), scales=scales[:], in_=hb[:])
-            h_codes[b, h] = codes
-            h_sc[b, h] = scales
+            return acc
 
-        w3_codes = []
-        w3_sc = []
+        def utterances(u):
+            return [(picked[a, u], picked_scales[a, u]) for a in range(2)]
 
-        def quantise_w3(a, round_copy):
-            wb = ring.tile([P, PACK * HALF], BF16, name="rounded", tag="rounded", bufs=4, align_bytes=64)
-            round_copy(
-                wb[:].rearrange("p (t m i) -> p m t i", t=PACK, i=PACK),
+        def hidden(b, u):
+            activated = ring.tile([P, PACK, HALF], F32, name="activated", tag="activated", bufs=4)
+            for t in range(PACK):
+                places = [H * a + PASS * b + P * t for a in range(2)]
+                columns = [
+                    (w1[:, 2 * first : 2 * (first + P)].bitcast(E2M1), w1_dealt_scales[:, first : first + P])
+                    for first in places
+                ]
+                nc.scalar.activation(activated[:, t, :], product(columns, utterances(u))[:], ACT.Gelu_apprx_tanh)
+            rounded = rounded_tile()
+            nc.vector.tensor_tensor(
+                interleaved(rounded[:]), by_slices(activated[:]), by_slices(paces[b, u][:]), ALU.mult
+            )
+            return rounded
+
+        def round_w3(a, copy):
+            rounded = rounded_tile()
+            copy(
+                rounded[:].rearrange("p (t m i) -> p m t i", t=PACK, i=PACK),
                 w3_raw[a][:].rearrange("p i (m t) -> p m t i", t=PACK),
             )
-            codes = keep.tile([P, N], U32, name="w3_codes%d" % a, align_bytes=64)
-            scales = keep.tile([P, N], U8, name="w3_sc%d" % a, align_bytes=64)
-            nc.vector.quantize_mx(out=codes[:].bitcast(E4M3), scales=scales[:], in_=wb[:])
-            w3_codes.append(codes)
-            w3_sc.append(scales)
+            return rounded
 
-        quantise_w3(0, nc.vector.tensor_copy)
+        w3_rounded = round_w3(0, nc.vector.tensor_copy)
         w2_raw = staged([P, 2 * N], I32, "w2_raw", 32)
         nc.sync.dma_start(
             w2_raw[:].rearrange("p (a c) -> p a c", a=2),
             w2_words.rearrange("a p c i -> p a (c i)").bitcast(I32),
         )
-        w2_sc_raw = staged([P, N], U8, "w2_sc_raw", 36)
-        nc.gpsimd.memset(w2_sc_raw[:].bitcast(I32), 0)
+        w2_scales_raw = staged([P, N], U8, "w2_scales_raw", 36)
+        nc.gpsimd.memset(w2_scales_raw[:].bitcast(I32), 0)
         for q in range(4):
             nc.sync.dma_start(
-                w2_sc_raw[32 * q : 32 * q + 8, :].bitcast(I32), w2_scales[:, 4 * q : 4 * q + 4, :].bitcast(I32)
+                w2_scales_raw[32 * q : 32 * q + 8, :].bitcast(I32), w2_scales[:, 4 * q : 4 * q + 4, :].bitcast(I32)
             )
 
+        h_rounded = {(0, 0): hidden(0, 0)}
+        h_mx = {}
 
-        hidden(0, 0)
-        load_wgo(0, 48)
-        hidden(1, 0)
-        load_wgo(1, 0)
-        hidden(0, 1)
-        quantise_w3(1, nc.scalar.copy)
-        hidden(1, 1)
-        x0_rows = x0.rearrange("(p t) m -> p t m", t=PACK)
-        y_rows = out_0.rearrange("(p t) m -> p t m", t=PACK)
+        def quantise_h(b, u):
+            h_mx[b, u] = quantise(h_rounded[b, u], "h%d%d" % (b, u))
 
-        w2 = keep.tile([P, 2 * N], I32, name="w2", align_bytes=64)
+        w3_mx = [quantise(w3_rounded, "w3_0")]
+        h_rounded[1, 0] = hidden(1, 0)
+        quantise_h(0, 0)
+        load_wgo(0, 0, 1, 8)
+        load_wgo(0, 1, 1, 14)
+        load_wgo(0, 2, 2, 10)
+        h_rounded[0, 1] = hidden(0, 1)
+        quantise_h(1, 0)
+        load_wgo(1, 0, PACK, 48)
+        w3_mx.append(quantise(round_w3(1, nc.scalar.copy), "w3_1"))
+        h_rounded[1, 1] = hidden(1, 1)
+
+        w2 = staged([P, 2 * N], I32, "w2", 24)
         nc.vector.tensor_copy(
-            w2[:].rearrange("p (a t c i) -> p a c t i", a=2, t=PACK, i=4),
-            w2_raw[:].rearrange("p (a c i t) -> p a c t i", a=2, t=PACK, i=4),
+            w2[:].rearrange("p (b t c i) -> p b c t i", b=2, t=PACK, i=4),
+            w2_raw[:].rearrange("p (b c i t) -> p b c t i", b=2, t=PACK, i=4),
         )
-        w2_sc = keep.tile([P, N], U8, name="w2_sc", align_bytes=64)
+        w2_dealt_scales = staged([P, N], U8, "w2_dealt_scales", 28)
         nc.vector.tensor_copy(
-            w2_sc[:].rearrange("p (t m) -> p t m", t=PACK),
-            w2_sc_raw[:].rearrange("p (m t) -> p t m", t=PACK),
+            w2_dealt_scales[:].rearrange("p (t m) -> p t m", t=PACK),
+            w2_scales_raw[:].rearrange("p (m t) -> p t m", t=PACK),
         )
 
+        units = [(t, u) for u in range(2) for t in range(PACK)]
         pages = [keep.tile([P, S], F32, name="page%d" % t) for t in range(PACK)]
 
-        def gated_weight(n, t, h):
-            gate = psum.tile([P, HALF], F32, name="acc", tag="acc")
-            for a in range(2):
-                nc.tensor.matmul_mx(
-                    out=gate[:],
-                    lhsT=w3_codes[a][:, P * t : P * (t + 1)].bitcast(E4M3),
-                    lhsT_scale=w3_sc[a][:, P * t : P * (t + 1)],
-                    rhs=v[a, h][:].bitcast(E4M3),
-                    rhs_scale=v_scales(a, h),
-                    start=(a == 0),
-                    stop=(a == 1),
-                )
+        def weigh_gate(n):
+            t, u = units[n]
+            cols = slice(P * t, P * (t + 1))
+            columns = [(codes[:, cols].bitcast(E4M3), scales[:, cols]) for codes, scales in w3_mx]
+            logits = product(columns, utterances(u))
             if n == 0:
-                th = keep.tile([P, HALF], F32, name="gate_first")
+                gate = keep.tile([P, HALF], F32, name="gate0")
             else:
-                th = staged([P, HALF], F32, "gate%d" % n, 24 + 2 * ((n - 1) % 4))
-            nc.scalar.activation(th[:], gate[:], ACT.Tanh, scale=0.5)
-            nc.scalar.activation(th[:], th[:], ACT.Copy, scale=0.5, bias=0.5)
-            weight = wgo_t[h][:, t, :]
-            (nc.gpsimd if n else nc.vector).tensor_tensor(weight, th[:], weight, ALU.mult)
-            return weight
+                gate = staged([P, HALF], F32, "gate%d" % n, 32 + 2 * ((n - 1) % GATE_SLOTS))
+            nc.scalar.activation(gate[:], logits[:], ACT.Tanh, scale=0.5)
+            nc.scalar.activation(gate[:], gate[:], ACT.Copy, scale=0.5, bias=0.5)
+            engine = nc.gpsimd if n else nc.vector
+            engine.tensor_tensor(weights[t, u], gate[:], weights[t, u], ALU.mult)
 
-        def correct(t, h, weight):
-            acc = psum.tile([P, HALF], F32, name="acc", tag="acc")
-            for b in range(2):
-                col = N * b + P * t
-                nc.tensor.matmul_mx(
-                    out=acc[:],
-                    lhsT=w2[:, col : col + P].bitcast(E4M3),
-                    lhsT_scale=w2_sc[4 * b :, P * t : P * (t + 1)],
-                    rhs=h_codes[b, h][:].bitcast(E4M3),
-                    rhs_scale=h_sc[b, h][:],
-                    start=(b == 0),
-                    stop=(b == 1),
-                )
-            if h == 0:
-                f = ring.tile([P, HALF], F32, name="f", tag="f", bufs=3)
-                nc.vector.tensor_tensor(f[:], weight, acc[:], ALU.mult)
+        def correction(n):
+            t, u = units[n]
+            columns = [
+                (w2[:, N * b + P * t : N * b + P * (t + 1)].bitcast(E4M3), w2_dealt_scales[4 * b :, P * t : P * (t + 1)])
+                for b in range(2)
+            ]
+            acc = product(columns, [h_mx[b, u] for b in range(2)])
+            values = keep.tile([P, HALF], F32, name="values%d" % n)
+            if n < VECTOR_UNITS:
+                nc.vector.tensor_tensor(values[:], weights[t, u], acc[:], ALU.mult)
             else:
-                f = ring.tile([P, HALF], F32, name="f_late", tag="f_late", bufs=4)
-                nc.scalar.copy(f[:], acc[:])
-                nc.gpsimd.tensor_tensor(f[:], f[:], weight, ALU.mult)
-            return f
+                nc.scalar.copy(values[:], acc[:])
+                nc.gpsimd.tensor_tensor(values[:], values[:], weights[t, u], ALU.mult)
+            return values
 
-        def put(t, h, f):
-            nc.vector.tensor_copy(pages[t][:].indirect(place[:, LIST_COLS * h : LIST_COLS * (h + 1)]), f[:])
-
-        def add_x0(engine, t, u):
-            cols = slice(HALF * u, HALF * (u + 1))
-            engine.tensor_tensor(y[u][:, t, :], pages[t][:, cols], y[u][:, t, :], ALU.add)
-            nc.sync.dma_start(y_rows[:, t, cols], y[u][:, t, :])
-
-        units = [(t, h) for h in range(2) for t in range(PACK)]
-        y = []
-        made = {}
+        def scatter(n, values):
+            t, u = units[n]
+            nc.vector.tensor_copy(pages[t][:].indirect(list_half(place, u)), values[:])
 
         def make(n):
-            made[n] = correct(*units[n], gated_weight(n, *units[n]))
+            weigh_gate(n)
+            return correction(n)
 
-        make(0)
-        put(*units[0], made[0])
-        make(1)
-        for n in range(1, len(units)):
-            if n + 1 < len(units):
-                make(n + 1)
-            put(*units[n], made[n])
+        weigh_gate(0)
+        quantise_h(0, 1)
+        first_values = correction(0)
+        quantise_h(1, 1)
+        scatter(0, first_values)
+        waiting = make(1)
+        for n in range(2, len(units)):
+            ahead = make(n)
+            scatter(n - 1, waiting)
+            waiting = ahead
+        scatter(len(units) - 1, waiting)
+
+        x0_rows = x0.rearrange("(p t) m -> p t m", t=PACK)
+        y_rows = out_0.rearrange("(p t) m -> p t m", t=PACK)
+        y = []
         for u in range(2):
-            tile = staged([P, PACK, HALF], F32, "y%d" % u, 44 + 8 * u)
-            nc.sync.dma_start(tile[:], x0_rows[:, :, HALF * u : HALF * (u + 1)])
+            tile = staged([P, PACK, HALF], F32, "y%d" % u, 4 + 8 * u)
+            nc.sync.dma_start(tile[:], x0_rows[:, :, half_cols(u)])
             y.append(tile)
-
-        for t in range(PACK - 1):
+        for t in range(PACK):
+            engine = nc.gpsimd if t < PACK - 1 else nc.vector
             for u in range(2):
-                add_x0(nc.gpsimd, t, u)
+                engine.tensor_tensor(y[u][:, t, :], pages[t][:, half_cols(u)], y[u][:, t, :], ALU.add)
+                nc.sync.dma_start(y_rows[:, t, half_cols(u)], y[u][:, t, :])
 
         y_codes = keep.tile([P, S], U32, name="y_codes", align_bytes=64)
-        y_sc = keep.tile([P, S], U8, name="y_sc", align_bytes=64)
+        y_scales = keep.tile([P, S], U8, name="y_scales", align_bytes=64)
         code_rows = out_1[0].rearrange("p m t -> p (m t)").bitcast(I32)
-        last = PACK - 1
-        quarter = S // 4
+        y_rounded = []
         for u in range(2):
-            add_x0(nc.vector, last, u)
-        for u in range(2):
-            cols = slice(HALF * u, HALF * (u + 1))
-            yb = ring.tile([P, PACK * HALF], BF16, name="rounded", tag="rounded", bufs=4, align_bytes=64)
-            for w in range(2):
-                c = 2 * u + w
-                mcols = slice(quarter * c, quarter * (c + 1))
-                dst = yb[:, PACK * quarter * w : PACK * quarter * (w + 1)]
-                dst_v = dst.rearrange("p (c i t) -> p c t i", i=2, t=PACK)
-                src_v = y[u][:, :, quarter * w : quarter * (w + 1)].rearrange("p t (c i) -> p c t i", i=2)
-                if w == 0:
-                    nc.scalar.copy(dst_v, src_v)
-                else:
-                    nc.vector.tensor_copy(dst_v, src_v)
-                nc.vector.quantize_mx(out=y_codes[:, mcols].bitcast(E4M3), scales=y_sc[:, mcols], in_=dst)
-            nc.sync.dma_start(code_rows[:, cols], y_codes[:, cols].bitcast(I32))
-        for q in range(4):
-            queue = nc.scalar if q % 2 else nc.sync
-            queue.dma_start(out_2[0, 4 * q : 4 * q + 4, :].bitcast(I32), y_sc[32 * q : 32 * q + 4, :].bitcast(I32))
+            rounded = rounded_tile()
+            for side, copy in enumerate((nc.scalar.copy, nc.vector.tensor_copy)):
+                part = rounded[:, PACK * QUARTER * side : PACK * QUARTER * (side + 1)]
+                copy(interleaved(part), by_slices(y[u][:, :, QUARTER * side : QUARTER * (side + 1)]))
+                y_rounded.append(part)
+        for u, quarters in enumerate(((0, 1), (3, 2))):
+            for quarter in quarters:
+                cols = slice(QUARTER * quarter, QUARTER * (quarter + 1))
+                nc.vector.quantize_mx(
+                    out=y_codes[:, cols].bitcast(E4M3), scales=y_scales[:, cols], in_=y_rounded[quarter]
+                )
+            nc.sync.dma_start(code_rows[:, half_cols(u)], y_codes[:, half_cols(u)].bitcast(I32))
+        for r in range(4):
+            queue = nc.scalar if r % 2 else nc.sync
+            queue.dma_start(out_2[0, r:16:4, :].bitcast(I32), y_scales[r:P:32, :].bitcast(I32))

from contextlib import ExitStack

import concourse.mybir as mybir

K, H, N, T, S = 1024, 1024, 512, 4096, 1024
FLOPS = 2 * S * (K * H + H * N + K * N)

F32 = mybir.dt.float32
BF16 = mybir.dt.bfloat16
I32 = mybir.dt.int32
U32 = mybir.dt.uint32
U16 = mybir.dt.uint16
U8 = mybir.dt.uint8
E4M3 = mybir.dt.float8_e4m3fn_x4
E2M1 = mybir.dt.float4_e2m1fn_x4
ACT = mybir.ActivationFunctionType
ALU = mybir.AluOpType

P = 128
PACK = 4
PASS = P * PACK
HALF = 512
QUARTER = S // 4
LIST_COLS = HALF // 16
KIB = 1024
GATE_SLOTS = 3
VECTOR_UNITS = 2


def tile_list_transcript_corrections_kernel(
    tc, tab_words, tab_scales, offs, w1_words, w1_scales, w2_words, w2_scales, w3, pace, wgo, offs2, x0,
    out_0, out_1, out_2,
):
    nc = tc.nc
    with ExitStack() as ctx:
        lists = ctx.enter_context(tc.tile_pool(name="lists", bufs=1))
        keep = ctx.enter_context(tc.tile_pool(name="keep", bufs=1))
        stage = ctx.enter_context(tc.tile_pool(name="stage", bufs=1))
        ring = ctx.enter_context(tc.tile_pool(name="ring", bufs=1))
        psum = ctx.enter_context(tc.psum_pool(name="psum", bufs=8))

        def staged(shape, dtype, name, at_kib):
            return stage.tile(shape, dtype, name=name, align_bytes=64, offset=at_kib * KIB)

        def half_cols(u):
            return slice(HALF * u, HALF * (u + 1))

        def list_half(tile, u):
            return tile[:, LIST_COLS * u : LIST_COLS * (u + 1)]

        def rounded_tile():
            return ring.tile([P, PACK * HALF], BF16, name="rounded", tag="rounded", bufs=4, align_bytes=64)

        def quantise(rounded, name):
            codes = keep.tile([P, HALF], U32, name=name + "_codes", align_bytes=64)
            scales = keep.tile([P, HALF], U8, name=name + "_scales", align_bytes=64)
            nc.vector.quantize_mx(out=codes[:].bitcast(E4M3), scales=scales[:], in_=rounded[:])
            return codes, scales

        def interleaved(rounded):
            return rounded.rearrange("p (c i t) -> p c t i", i=2, t=PACK)

        def by_slices(rows):
            return rows.rearrange("p t (c i) -> p c t i", i=2)

        def load_scale_rows(tile, rows):
            for r in range(4):
                nc.sync.dma_start(
                    tile[r:P:32, :].bitcast(I32).rearrange("p (a c) -> p a c", a=2),
                    rows[:, r:16:4, :].bitcast(I32).rearrange("a q c -> q a c"),
                )

        def load_table(a, at_kib):
            words = staged([P, T], I32, "table%d" % a, at_kib)
            nc.sync.dma_start(words[:], tab_words[a].rearrange("p t i -> p (t i)").bitcast(I32))
            return words

        def load_rows(rows, name, at_kib):
            tile = staged([P, PACK, HALF], F32, name, at_kib)
            nc.sync.dma_start(tile[:], rows.rearrange("(p t) c -> p t c", t=PACK))
            return tile

        def load_pace(b, u, at_kib):
            return load_rows(pace[PASS * b : PASS * (b + 1), half_cols(u)], "pace%d%d" % (b, u), at_kib)

        def load_w3(a, at_kib):
            return load_rows(w3[PASS * a : PASS * (a + 1), :], "w3_raw%d" % a, at_kib)

        wgo_rows = wgo.rearrange("(q t) j -> q t j", t=PACK)
        weights = {}

        def load_wgo(u, t0, count, at_kib):
            tile = staged([P, count, HALF], F32, "wgo%d%d" % (u, t0), at_kib)
            for q in (0, 2, 1, 3):
                nc.sync.dma_start(tile[32 * q : 32 * (q + 1), :, :], wgo_rows[:, t0 : t0 + count, half_cols(u)])
            for t in range(t0, t0 + count):
                weights[t, u] = tile[:, t - t0, :]

        pick = lists.tile([P, S // 16], U16, name="pick")
        place = lists.tile([P, S // 16], U16, name="place")

        table_scales = staged([P, 2 * T], U8, "table_scales", 48)
        w1_scales_raw = staged([P, 2 * H], U8, "w1_scales_raw", 40)
        w1_raw = staged([P, 2 * 2 * H], U8, "w1_raw", 30)
        nc.vector.memset(table_scales[:].bitcast(I32), 0)
        nc.gpsimd.memset(w1_scales_raw[:].bitcast(I32), 0)

        nc.sync.dma_start(pick[:], offs)
        nc.sync.dma_start(
            w1_raw[:].bitcast(I32).rearrange("p (a c) -> p a c", a=2),
            w1_words.bitcast(I32).rearrange("a p c -> p a c"),
        )
        table = [load_table(0, 0)]
        nc.sync.dma_start(place[:], offs2)
        load_scale_rows(w1_scales_raw, w1_scales)
        load_scale_rows(table_scales, tab_scales)

        w1 = keep.tile([P, 2 * 2 * H], U8, name="w1", align_bytes=64)
        nc.vector.tensor_copy(
            w1[:].rearrange("p (g t m e) -> p g t m e", t=PACK, m=P, e=2),
            w1_raw[:].rearrange("p (g m t e) -> p g t m e", t=PACK, m=P, e=2),
        )
        table.append(load_table(1, 16))
        w3_raw = [load_w3(0, 32)]
        w1_dealt_scales = keep.tile([P, 2 * H], U8, name="w1_dealt_scales", align_bytes=64)
        nc.vector.tensor_copy(
            w1_dealt_scales[:].rearrange("p (g t m) -> p g t m", t=PACK, m=P),
            w1_scales_raw[:].rearrange("p (g m t) -> p g t m", t=PACK, m=P),
        )

        picked = {}
        picked_scales = {}

        def gather_words(a, u):
            tile = keep.tile([P, HALF], U32, name="picked%d%d" % (a, u), align_bytes=64)
            nc.vector.tensor_copy(tile[:], table[a][:].bitcast(U32).indirect(list_half(pick, u)))
            picked[a, u] = tile

        def gather_scales(a, u):
            tile = keep.tile([P, HALF], U8, name="picked_scales%d%d" % (a, u), align_bytes=64)
            nc.vector.tensor_copy(tile[:], table_scales[:, T * a : T * (a + 1)].indirect(list_half(pick, u)))
            picked_scales[a, u] = tile

        paces = {}
        for u in range(2):
            gather_words(0, u)
        for u in range(2):
            for a in range(2):
                gather_scales(a, u)
        paces[0, 0] = load_pace(0, 0, 8)
        paces[1, 0] = load_pace(1, 0, 0)
        paces[0, 1] = load_pace(0, 1, 48)
        for u in range(2):
            gather_words(1, u)
        w3_raw.append(load_w3(1, 16))
        paces[1, 1] = load_pace(1, 1, 24)

        def product(stationary, moving):
            acc = psum.tile([P, HALF], F32, name="acc", tag="acc")
            for a in range(2):
                nc.tensor.matmul_mx(
                    out=acc[:],
                    lhsT=stationary[a][0],
                    lhsT_scale=stationary[a][1],
                    rhs=moving[a][0][:].bitcast(E4M3),
                    rhs_scale=moving[a][1][:],
                    start=(a == 0),
                    stop=(a == 1),
                )
            return acc

        def utterances(u):
            return [(picked[a, u], picked_scales[a, u]) for a in range(2)]

        def hidden(b, u):
            activated = ring.tile([P, PACK, HALF], F32, name="activated", tag="activated", bufs=4)
            for t in range(PACK):
                places = [H * a + PASS * b + P * t for a in range(2)]
                columns = [
                    (w1[:, 2 * first : 2 * (first + P)].bitcast(E2M1), w1_dealt_scales[:, first : first + P])
                    for first in places
                ]
                nc.scalar.activation(activated[:, t, :], product(columns, utterances(u))[:], ACT.Gelu_apprx_tanh)
            rounded = rounded_tile()
            nc.vector.tensor_tensor(
                interleaved(rounded[:]), by_slices(activated[:]), by_slices(paces[b, u][:]), ALU.mult
            )
            return rounded

        def round_w3(a, copy):
            rounded = rounded_tile()
            copy(
                rounded[:].rearrange("p (t m i) -> p m t i", t=PACK, i=PACK),
                w3_raw[a][:].rearrange("p i (m t) -> p m t i", t=PACK),
            )
            return rounded

        w3_rounded = round_w3(0, nc.vector.tensor_copy)
        w2_raw = staged([P, 2 * N], I32, "w2_raw", 32)
        nc.sync.dma_start(
            w2_raw[:].rearrange("p (a c) -> p a c", a=2),
            w2_words.rearrange("a p c i -> p a (c i)").bitcast(I32),
        )
        w2_scales_raw = staged([P, N], U8, "w2_scales_raw", 36)
        nc.gpsimd.memset(w2_scales_raw[:].bitcast(I32), 0)
        for q in range(4):
            nc.sync.dma_start(
                w2_scales_raw[32 * q : 32 * q + 8, :].bitcast(I32), w2_scales[:, 4 * q : 4 * q + 4, :].bitcast(I32)
            )

        h_rounded = {(0, 0): hidden(0, 0)}
        h_mx = {}

        def quantise_h(b, u):
            h_mx[b, u] = quantise(h_rounded[b, u], "h%d%d" % (b, u))

        w3_mx = [quantise(w3_rounded, "w3_0")]
        h_rounded[1, 0] = hidden(1, 0)
        quantise_h(0, 0)
        load_wgo(0, 0, 1, 8)
        load_wgo(0, 1, 1, 14)
        load_wgo(0, 2, 2, 10)
        h_rounded[0, 1] = hidden(0, 1)
        quantise_h(1, 0)
        load_wgo(1, 0, PACK, 48)
        w3_mx.append(quantise(round_w3(1, nc.scalar.copy), "w3_1"))
        h_rounded[1, 1] = hidden(1, 1)

        w2 = staged([P, 2 * N], I32, "w2", 24)
        nc.vector.tensor_copy(
            w2[:].rearrange("p (b t c i) -> p b c t i", b=2, t=PACK, i=4),
            w2_raw[:].rearrange("p (b c i t) -> p b c t i", b=2, t=PACK, i=4),
        )
        w2_dealt_scales = staged([P, N], U8, "w2_dealt_scales", 28)
        nc.vector.tensor_copy(
            w2_dealt_scales[:].rearrange("p (t m) -> p t m", t=PACK),
            w2_scales_raw[:].rearrange("p (m t) -> p t m", t=PACK),
        )

        units = [(t, u) for u in range(2) for t in range(PACK)]
        pages = [keep.tile([P, S], F32, name="page%d" % t) for t in range(PACK)]

        def weigh_gate(n):
            t, u = units[n]
            cols = slice(P * t, P * (t + 1))
            columns = [(codes[:, cols].bitcast(E4M3), scales[:, cols]) for codes, scales in w3_mx]
            logits = product(columns, utterances(u))
            if n == 0:
                gate = keep.tile([P, HALF], F32, name="gate0")
            else:
                gate = staged([P, HALF], F32, "gate%d" % n, 32 + 2 * ((n - 1) % GATE_SLOTS))
            nc.scalar.activation(gate[:], logits[:], ACT.Tanh, scale=0.5)
            nc.scalar.activation(gate[:], gate[:], ACT.Copy, scale=0.5, bias=0.5)
            engine = nc.gpsimd if n else nc.vector
            engine.tensor_tensor(weights[t, u], gate[:], weights[t, u], ALU.mult)

        def correction(n):
            t, u = units[n]
            columns = [
                (w2[:, N * b + P * t : N * b + P * (t + 1)].bitcast(E4M3), w2_dealt_scales[4 * b :, P * t : P * (t + 1)])
                for b in range(2)
            ]
            acc = product(columns, [h_mx[b, u] for b in range(2)])
            values = keep.tile([P, HALF], F32, name="values%d" % n)
            if n < VECTOR_UNITS:
                nc.vector.tensor_tensor(values[:], weights[t, u], acc[:], ALU.mult)
            else:
                nc.scalar.copy(values[:], acc[:])
                nc.gpsimd.tensor_tensor(values[:], values[:], weights[t, u], ALU.mult)
            return values

        def scatter(n, values):
            t, u = units[n]
            nc.vector.tensor_copy(pages[t][:].indirect(list_half(place, u)), values[:])

        def make(n):
            weigh_gate(n)
            return correction(n)

        weigh_gate(0)
        quantise_h(0, 1)
        first_values = correction(0)
        quantise_h(1, 1)
        scatter(0, first_values)
        waiting = make(1)
        for n in range(2, len(units)):
            ahead = make(n)
            scatter(n - 1, waiting)
            waiting = ahead
        scatter(len(units) - 1, waiting)

        x0_rows = x0.rearrange("(p t) m -> p t m", t=PACK)
        y_rows = out_0.rearrange("(p t) m -> p t m", t=PACK)
        y = []
        for u in range(2):
            tile = staged([P, PACK, HALF], F32, "y%d" % u, 4 + 8 * u)
            nc.sync.dma_start(tile[:], x0_rows[:, :, half_cols(u)])
            y.append(tile)
        for t in range(PACK):
            engine = nc.gpsimd if t < PACK - 1 else nc.vector
            for u in range(2):
                engine.tensor_tensor(y[u][:, t, :], pages[t][:, half_cols(u)], y[u][:, t, :], ALU.add)
                nc.sync.dma_start(y_rows[:, t, half_cols(u)], y[u][:, t, :])

        y_codes = keep.tile([P, S], U32, name="y_codes", align_bytes=64)
        y_scales = keep.tile([P, S], U8, name="y_scales", align_bytes=64)
        code_rows = out_1[0].rearrange("p m t -> p (m t)").bitcast(I32)
        y_rounded = []
        for u in range(2):
            rounded = rounded_tile()
            for side, copy in enumerate((nc.scalar.copy, nc.vector.tensor_copy)):
                part = rounded[:, PACK * QUARTER * side : PACK * QUARTER * (side + 1)]
                copy(interleaved(part), by_slices(y[u][:, :, QUARTER * side : QUARTER * (side + 1)]))
                y_rounded.append(part)
        for u, quarters in enumerate(((0, 1), (3, 2))):
            for quarter in quarters:
                cols = slice(QUARTER * quarter, QUARTER * (quarter + 1))
                nc.vector.quantize_mx(
                    out=y_codes[:, cols].bitcast(E4M3), scales=y_scales[:, cols], in_=y_rounded[quarter]
                )
            nc.sync.dma_start(code_rows[:, half_cols(u)], y_codes[:, half_cols(u)].bitcast(I32))
        for r in range(4):
            queue = nc.scalar if r % 2 else nc.sync
            queue.dma_start(out_2[0, r:16:4, :].bitcast(I32), y_scales[r:P:32, :].bitcast(I32))
